import numpy as np, ml_dtypes
CORES = [88,96,104,112,120,216,224,232,240,248]
N = 10
import mx_ref
NC, KT, WT = 128, 4, 1
BF = ml_dtypes.bfloat16
def cut(t, i, w=512):
    return t[:, w * i:w * i + w]
def pk(c, s, i=0):
    return (np.ascontiguousarray(c[:, 512 * i:512 * i + 512]), mx_ref.live(s[:, 128 * i:128 * i + 128]))
def inputs(rng, e, E):
    def f(*shape):
        v = (rng.standard_normal(shape, dtype=np.float32) * np.exp2(rng.integers(-2, 3, shape[:-1] + (1,)))).astype(BF)
        return mx_ref.spread((v.astype(np.float32) * np.exp2(rng.integers(-E, E + 1, shape[:-2] + (1, 1))).astype(np.float32)).astype(BF), rng, e)
    def packed(k):
        c = np.zeros((N, 128, k * 512), np.uint8); s = np.zeros((N, 128, k * 128), np.uint8)
        for r in range(N):
            for i in range(k):
                a, b = mx_ref.quantize(f(128, 512)); c[r][:, 512 * i:512 * i + 512] = a; s[r][:, 128 * i:128 * i + 128] = mx_ref.plane(b, rng)
        return c, s
    d = {}
    d["wc"], d["ws"] = packed(KT * WT)
    d["x"] = f(N, 128, KT * 4 * NC)
    return d
def setup_inputs(rng):
    return inputs(rng, 0, 0)
def setup_inputs_blocks(rng):
    return inputs(rng, 2, 0)
def setup_inputs_wide(rng):
    d = inputs(rng, 0, 1); d["x"] = inputs(rng, 0, 0)["x"]
    return d
def reference(wc, ws, x):
    X = [[mx_ref.quantize(cut(x[j], t, 4 * NC)) for t in range(KT)] for j in range(N)]
    y = np.zeros((N, 128, N * WT * NC), np.float32)
    for r in range(N):
        for b in range(N * WT):
            j, i = divmod(b, WT)
            for t in range(KT):
                p = mx_ref.matmul(pk(wc[r], ws[r], KT * i + t), X[j][t])
                z = p if t == 0 else z + p
            y[r][:, NC * b:NC * b + NC] = z
    return {"y": y}

@@ -1,0 +1,353 @@
+from concourse.bass import DstId, RemoteDMATransfer
+from concourse.mybir import dt
+
+N = 10
+KT = 4
+W = 128
+SIM = 256
+NSLOT = 7
+NPL = 4
+NY = 2
+NBANK = 8
+NEAR = 2
+
+SCRATCH = {
+    "xs": ("sbuf", [128, 2 * 4 * W], "bfloat16"),
+    "wq": ("sbuf", [128, KT * W], "float8_e4m3fn_x4"),
+    "wp": ("sbuf", [128, KT * W], "uint8"),
+    "cq": ("sbuf", [128, NSLOT * W], "float8_e4m3fn_x4"),
+    "cp": ("sbuf", [128, NPL * 2 * W], "uint8"),
+    "yb": ("sbuf", [128, NY * W], "float32"),
+    "ps": ("psum", [128, 512 * NBANK], "float32"),
+}
+for _i in range(N - 1):
+    for _w in range(2):
+        SCRATCH["q%d_%d" % (_i, _w)] = ("dram", [128, 2 * W], "float8_e4m3fn_x4")
+    SCRATCH["p%d_0" % _i] = ("dram", [128, KT * W], "uint8")
+
+SEMAPHORES = (["x%d" % t for t in range(KT)] + ["wld", "qz", "mm", "ev", "sent", "fo0", "fo1", "fp0"]
+              + ["ls%d" % c for c in range(NSLOT)] + ["pl%d" % c for c in range(NPL)] + ["ys%d" % c for c in range(NY)]
+              + ["aq%d_%d" % (s, w) for s in range(N) for w in range(2)] + ["ap%d_0" % s for s in range(N)])
+
+
+def ones(mask):
+    return bin(mask).count("1")
+
+
+def chip_of(topo, c):
+    return (topo.host(c), topo.chip(c))
+
+
+def idx(s, d):
+    return (s - d - 1) % N
+
+
+_memo = {}
+
+
+def plan(topo, cores):
+    if "p" in _memo:
+        return _memo["p"]
+    chips = {}
+    for c in range(SIM):
+        chips.setdefault(chip_of(topo, c), []).append(c)
+    home = {chip_of(topo, c): r for r, c in enumerate(cores)}
+    mate = [None] * N
+    mchip = [None] * N
+    for r, c in enumerate(cores):
+        mchip[r] = chip_of(topo, [k for k in range(SIM) if topo.mates(c, k)][0])
+        mate[r] = home.get(mchip[r])
+    serves = dict(home)
+    for r in range(N):
+        if mate[r] is None:
+            serves[mchip[r]] = r
+    gate = {}
+    for ch, r in serves.items():
+        over = chips[mchip[r]][0] if ch in home else cores[r]
+        gate[ch] = [[], []]
+        for c in chips[ch]:
+            if c not in cores and topo.may_write(c, over):
+                gate[ch][topo.die(c) != topo.die(cores[r])].append(c)
+    same = [[topo.same_plane(cores[s], cores[d]) for d in range(N)] for s in range(N)]
+    nxt = [[d for d in [(s + k) % N for k in range(1, N)] if same[s][d]][:NEAR] for s in range(N)]
+    early = [[s for s in [(d - k) % N for k in range(1, N)] if d in nxt[s]] for d in range(N)]
+    direct = [[] for _ in range(N)]
+    first = [[] for _ in range(N)]
+    relays = {ch: [] for ch in serves}
+    for s in range(N):
+        ring = [(s + k) % N for k in range(1, N)]
+        if mate[s] is None:
+            direct[s] = [[d for d in ring if not same[s][d]], [d for d in ring if same[s][d] and d not in nxt[s]]]
+            continue
+        direct[s] = [[mate[s]] + [d for d in ring if same[s][d] and mate[d] is None and d not in nxt[s]]]
+        for d in ring:
+            if mate[d] is not None and same[s][d]:
+                first[s].append(chip_of(topo, cores[d]))
+                relays[first[s][-1]].append((s, [mate[d]] + ([d] if d not in nxt[s] else [])))
+            elif mate[d] is None and not same[s][d]:
+                first[s].append(mchip[d])
+                relays[mchip[d]].append((s, [d]))
+    for ch, lst in relays.items():
+        lst.sort(key=lambda e: (serves[ch] - e[0]) % N)
+    alias = {}
+    for ch, r in home.items():
+        used = [s for s, _ in relays[ch]]
+        alias[ch] = idx([s for s in range(N) if s != r and s not in used][0], r)
+    order = []
+    for d in range(N):
+        soon = [s for s in range(N) if s not in early[d] and any(d in l for l in direct[s])]
+        soon.sort(key=lambda s: (s != mate[d], (d - s) % N))
+        late = [s for s in range(N) if s != d and s not in early[d] and s not in soon]
+        late.sort(key=lambda s: (not same[s][d], (d - s) % N))
+        items = [(d, 0), (d, 1)] + [(s, w) for w in range(2) for s in early[d]]
+        for s in soon + late:
+            items += [(s, 0), (s, 1)]
+        order.append(items)
+    _memo["p"] = {"home": home, "mate": mate, "serves": serves, "gate": gate, "same": same, "direct": direct,
+                  "first": first, "relays": relays, "alias": alias, "order": order, "nxt": nxt, "early": early}
+    return _memo["p"]
+
+
+def side(s, w):
+    return (s + w) % 2
+
+
+def rank_program(g, core, T, topo):
+    P = plan(topo, T.cores)
+    ch = chip_of(topo, core)
+    if ch not in P["serves"]:
+        return
+    if T.rank_of(core) is None:
+        helper_program(g, core, T, topo, P, ch)
+    else:
+        rank_core_program(g, core, T, topo, P, ch)
+
+
+def view(T, kind, i, u):
+    b = T["%s%d_%d" % (kind, i, u)]
+    return b[:].bitcast(dt.uint8) if kind == "q" else b[:]
+
+
+def transfer(core, T, topo, kind, s, u, src, dests, mask):
+    ids = []
+    for c, _ in dests:
+        rid, pid = topo.addr(c, core)
+        ids.append(DstId(rid=rid, pnc=pid))
+    return RemoteDMATransfer(dst_ids=ids, dma_engine_mask=mask, remote_sem=T.sem["a%s%d_%d" % (kind, s, u)],
+                             srcs=[src], dsts=[v for _, v in dests])
+
+
+def off_chip(topo, cores):
+    return topo.mask(cores[0], [c for c in cores if topo.same_plane(cores[0], c)][0])
+
+
+def helper_jobs(P, ch):
+    jobs = {}
+    gate = P["gate"][ch]
+    me = P["home"].get(ch)
+
+    def add(c, *job):
+        jobs.setdefault(c, []).append(job)
+
+    if me is not None:
+        others = [(me + k) % N for k in range(1, N)]
+        same = [d for d in others if P["same"][me][d] and d not in P["nxt"][me]]
+        cross = [d for d in others if not P["same"][me][d]]
+        for w in range(2):
+            groups = [[("rank", d) for d in l] for l in P["direct"][me]] + [[("relay", c) for c in P["first"][me]]]
+            add(gate[side(me, w)][0], "send", "q", w, [grp for grp in groups if grp])
+        add(gate[side(me, 1)][1], "send", "p", 0, [[("rank", d) for d in cross]])
+        if same:
+            add(gate[side(me, 0)][1], "send", "p", 0, [[("rank", d) for d in same]])
+    for w in range(2):
+        for s, ranks in P["relays"][ch]:
+            add(gate[side(s, w)][1], "relay", "q", w, s, ranks)
+    return jobs
+
+
+def handed(P, ch, kind, w):
+    return [c for c, js in sorted(helper_jobs(P, ch).items()) if any(j[:3] == ("send", kind, w) for j in js)]
+
+
+def helper_program(g, core, T, topo, P, ch):
+    cores = T.cores
+    me = P["serves"][ch]
+    off = off_chip(topo, cores)
+    sent = [0]
+
+    def call(trs):
+        g.remote_dma_fused(trs, local_sem=T.sem.sent)
+        sent[0] += ones(off) * len(trs)
+
+    for job in helper_jobs(P, ch).get(core, []):
+        if job[0] == "send":
+            _, kind, w, groups = job
+            src = view(T, kind, P["alias"][ch], w)
+            g.wait_ge(T.sem["a%s%d_%d" % (kind, me, w)], ones(off))
+            for grp in groups:
+                dests = []
+                for to, d in grp:
+                    if to == "rank":
+                        dests.append((cores[d], view(T, kind, idx(me, d), w)))
+                    else:
+                        dests.append((P["gate"][d][side(me, w)][1], view(T, kind, idx(me, P["serves"][d]), w)))
+                call([transfer(core, T, topo, kind, me, w, src, dests, topo.mask(core, dests[0][0]) & off)])
+        else:
+            _, kind, w, s, ranks = job
+            src = view(T, kind, idx(s, me), w)
+            g.wait_ge(T.sem["a%s%d_%d" % (kind, s, w)], ones(off))
+            trs = []
+            for d in ranks:
+                m = topo.mask(core, cores[d])
+                trs.append(transfer(core, T, topo, kind, s, w, src, [(cores[d], view(T, kind, idx(s, d), w))],
+                                    m if m == off else m & ~off))
+            call(trs)
+    if sent[0]:
+        g.wait_ge(T.sem.sent, sent[0])
+
+
+def rank_core_program(g, core, T, topo, P, ch):
+    cores = T.cores
+    me = T.rank_of(core)
+    al = P["alias"][ch]
+    off = off_chip(topo, cores)
+    full = ones(off)
+    S = T.sem
+    items = P["order"][me]
+    lead = P["early"][me][0]
+    nxt = P["nxt"][me]
+
+    def cspan(c, n=1):
+        return T.cq[:, c * W:(c + n) * W]
+
+    def pspan(c, n=1):
+        return T.cp[:, 2 * c * W:2 * (c + n) * W]
+
+    def ptile(c, h):
+        return T.cp[:, (2 * c + h) * W:(2 * c + h + 1) * W]
+
+    def xcols(t):
+        return T.xs[:, (t % 2) * 4 * W:(t % 2 + 1) * 4 * W]
+
+    def xload(q, t):
+        q.dma_start(xcols(t), T.x[:, t * 4 * W:(t + 1) * 4 * W]).then_inc(S["x%d" % t], 16)
+
+    xload(g.sync, 0)
+    xload(g.scalar, 1)
+    g.sync.dma_start(T.wq[:].bitcast(dt.uint8), T.wc[:]).then_inc(S.wld, 16)
+    g.scalar.dma_start(T.wp[:], T.ws[:]).then_inc(S.wld, 16)
+    for t in range(KT):
+        g.vector.wait_ge(S["x%d" % t], 16)
+        g.vector.quantize_mx(cspan(t), ptile(t // 2, t % 2), xcols(t)).then_inc(S.qz, 1)
+    g.sync.wait_ge(S.qz, 1)
+    xload(g.sync, 2)
+    g.scalar.wait_ge(S.qz, 2)
+    xload(g.scalar, 3)
+
+    fo = {}
+    for kind, w in (("q", 0), ("p", 0), ("q", 1)):
+        g.wait_ge(S.qz, 2 if (kind, w) == ("q", 0) else KT)
+        if kind == "q":
+            src, sem = cspan(2 * w, 2).bitcast(dt.uint8), "fo%d" % w
+        else:
+            src, sem = pspan(0, 2), "fp0"
+        hs = handed(P, ch, kind, w)
+        trs = [transfer(core, T, topo, kind, me, w, src, [(h, view(T, kind, al, w)) for h in hs], topo.mask(core, hs[0]) & ~off)]
+        dests = []
+        for d in nxt:
+            land = view(T, kind, idx(me, d), w)
+            if P["early"][d][0] == me and (kind, w) == ("q", 0):
+                land = cspan(KT, 2).bitcast(dt.uint8)
+            if P["early"][d][0] == me and kind == "p":
+                land = pspan(2, 2)
+            dests.append((cores[d], land))
+        trs.append(transfer(core, T, topo, kind, me, w, src, dests, off))
+        g.remote_dma_fused(trs, local_sem=S[sem])
+        fo[sem] = full * len(trs)
+
+    srcs = [s for s, w in items if w == 0]
+    done = [s for s, w in items if w == 1]
+    bank = {s: k % NBANK for k, s in enumerate(srcs)}
+    last = {s: 2 * items.index((s, 1)) + 2 for s in srcs}
+    pl, before = {}, {}
+    for i, (s, w) in enumerate(items):
+        if s == me:
+            pl[i] = w
+        elif s == lead:
+            pl[i] = 2 + w
+    queue = [i for i in range(2)]
+    for i, (s, w) in enumerate(items):
+        if s == lead:
+            queue.append(i)
+        elif s != me:
+            before[i] = queue.pop(0)
+            pl[i] = pl[before[i]]
+            queue.append(i)
+
+    uses, need, pneed = {}, {}, {}
+
+    def load(sem, out, in_):
+        g.sync.dma_start(out, in_).then_inc(S[sem], 16)
+        uses[sem] = uses.get(sem, 0) + 16
+        return (sem, uses[sem])
+
+    for i, (s, w) in enumerate(items):
+        if s == me:
+            continue
+        if s == lead:
+            pneed[i] = ("ap%d_0" % s, full)
+        else:
+            g.sync.wait_ge(S.mm, 2 * before[i] + 2)
+            if before[i] < 2:
+                g.sync.wait_ge(S.fp0, fo["fp0"])
+            g.sync.wait_ge(S["ap%d_0" % s], full)
+            pneed[i] = load("pl%d" % pl[i], pspan(pl[i]), T["p%d_0" % idx(s, me)][:, 2 * w * W:2 * (w + 1) * W])
+        n = 2 * i
+        if s == lead and w == 0:
+            need[n] = need[n + 1] = ("aq%d_%d" % (s, w), full)
+            continue
+        src = T["q%d_%d" % (idx(s, me), w)]
+        pieces = [(0, 2)] if n % NSLOT + 1 < NSLOT else [(0, 1), (1, 1)]
+        g.sync.wait_ge(S["aq%d_%d" % (s, w)], full)
+        for h, m in pieces:
+            lo, hi = n + h - NSLOT, n + h + m - NSLOT
+            if hi > 0:
+                g.sync.wait_ge(S.mm, hi)
+            for u in range(2):
+                if max(lo, 2 * u) < min(hi, 2 * u + 2):
+                    g.sync.wait_ge(S["fo%d" % u], fo["fo%d" % u])
+            c = (n + h) % NSLOT
+            nd = load("ls%d" % c, cspan(c, m).bitcast(dt.uint8), src[:, h * W:(h + m) * W].bitcast(dt.uint8))
+            for b in range(m):
+                need[n + h + b] = nd
+
+    g.tensor.wait_ge(S.wld, 32)
+    for i, (s, w) in enumerate(items):
+        k = srcs.index(s)
+        if s == me:
+            g.tensor.wait_ge(S.qz, 2 * w + 2)
+        else:
+            g.tensor.wait_ge(S[pneed[i][0]], pneed[i][1])
+        if w == 0 and k >= NBANK:
+            g.tensor.wait_ge(S.ev, done.index(srcs[k - NBANK]) + 1)
+        for h in range(2):
+            t = 2 * w + h
+            n = 2 * i + h
+            if s != me and (h == 0 or need[n] != need[n - 1]):
+                g.tensor.wait_ge(S[need[n][0]], need[n][1])
+            g.tensor.matmul_mx(T.ps[:, 512 * bank[s]:512 * bank[s] + W], T.wq[:, t * W:(t + 1) * W], T.wp[:, t * W:(t + 1) * W],
+                               cspan(n % NSLOT), ptile(pl[i], h), t == 0, t == KT - 1).then_inc(S.mm, 1)
+
+    for k, j in enumerate(done):
+        c = k % NY
+        g.vector.wait_ge(S.mm, last[j])
+        if k >= NY:
+            g.vector.wait_ge(S["ys%d" % c], 16 * (k // NY))
+        g.vector.tensor_copy(T.yb[:, c * W:(c + 1) * W], T.ps[:, 512 * bank[j]:512 * bank[j] + W]).then_inc(S.ev, 1)
+        g.scalar.wait_ge(S.ev, k + 1)
+        g.scalar.dma_start(T.y[:, j * W:(j + 1) * W], T.yb[:, c * W:(c + 1) * W]).then_inc(S["ys%d" % c], 16)
+
+    for c in range(NY):
+        g.scalar.wait_ge(S["ys%d" % c], 16 * len([k for k in range(N) if k % NY == c]))
+    for sem in fo:
+        g.wait_ge(S[sem], fo[sem])

@@ -5,18 +5,21 @@ N = 10
 KT = 4
 W = 128
 SIM = 256
-NSLOT = 7
-NPL = 4
+NSLOT = 6
+NPL = 3
 NY = 2
 NBANK = 8
 NEAR = 2
+
+PARTS = [("q", 0), ("p", 0), ("q", 1)]
+CALLS = [("q", 0, True), ("p", 0, True), ("q", 1, True), ("p", 0, False), ("q", 0, False), ("q", 1, False)]
 
 SCRATCH = {
     "xs": ("sbuf", [128, 2 * 4 * W], "bfloat16"),
     "wq": ("sbuf", [128, KT * W], "float8_e4m3fn_x4"),
     "wp": ("sbuf", [128, KT * W], "uint8"),
     "cq": ("sbuf", [128, NSLOT * W], "float8_e4m3fn_x4"),
-    "cp": ("sbuf", [128, NPL * 2 * W], "uint8"),
+    "cp": ("sbuf", [128, NPL * KT * W], "uint8"),
     "yb": ("sbuf", [128, NY * W], "float32"),
     "ps": ("psum", [128, 512 * NBANK], "float32"),
 }
@@ -25,9 +28,9 @@ for _i in range(N - 1):
         SCRATCH["q%d_%d" % (_i, _w)] = ("dram", [128, 2 * W], "float8_e4m3fn_x4")
     SCRATCH["p%d_0" % _i] = ("dram", [128, KT * W], "uint8")
 
-SEMAPHORES = (["x%d" % t for t in range(KT)] + ["wld", "qz", "mm", "ev", "sent", "fo0", "fo1", "fp0"]
+SEMAPHORES = (["x%d" % t for t in range(KT)] + ["wld", "qz", "mm", "ev", "sent"] + ["f%s%d" % p for p in PARTS]
               + ["ls%d" % c for c in range(NSLOT)] + ["pl%d" % c for c in range(NPL)] + ["ys%d" % c for c in range(NY)]
-              + ["aq%d_%d" % (s, w) for s in range(N) for w in range(2)] + ["ap%d_0" % s for s in range(N)])
+              + ["a%s%d_%d" % (k, s, u) for s in range(N) for k, u in PARTS])
 
 
 def ones(mask):
@@ -51,180 +54,105 @@ def plan(topo, cores):
     chips = {}
     for c in range(SIM):
         chips.setdefault(chip_of(topo, c), []).append(c)
-    home = {chip_of(topo, c): r for r, c in enumerate(cores)}
-    mate = [None] * N
-    mchip = [None] * N
-    for r, c in enumerate(cores):
-        mchip[r] = chip_of(topo, [k for k in range(SIM) if topo.mates(c, k)][0])
-        mate[r] = home.get(mchip[r])
-    serves = dict(home)
-    for r in range(N):
-        if mate[r] is None:
-            serves[mchip[r]] = r
-    gate = {}
-    for ch, r in serves.items():
-        over = chips[mchip[r]][0] if ch in home else cores[r]
-        gate[ch] = [[], []]
-        for c in chips[ch]:
-            if c not in cores and topo.may_write(c, over):
-                gate[ch][topo.die(c) != topo.die(cores[r])].append(c)
-    same = [[topo.same_plane(cores[s], cores[d]) for d in range(N)] for s in range(N)]
-    nxt = [[d for d in [(s + k) % N for k in range(1, N)] if same[s][d]][:NEAR] for s in range(N)]
-    early = [[s for s in [(d - k) % N for k in range(1, N)] if d in nxt[s]] for d in range(N)]
-    direct = [[] for _ in range(N)]
-    first = [[] for _ in range(N)]
-    relays = {ch: [] for ch in serves}
+    ring = [[(s + k) % N for k in range(1, N)] for s in range(N)]
+    plane = [[d for d in ring[s] if topo.same_plane(cores[s], cores[d])] for s in range(N)]
+    nxt = [plane[s][:NEAR] for s in range(N)]
+    early = [[[s for s in range(N) if nxt[s][k] == d][0] for k in range(NEAR)] for d in range(N)]
+    third = [plane[s][NEAR:NEAR + 1] for s in range(N)]
+    far = [third[s] + [d for d in ring[s] if d not in nxt[s] + third[s]] for s in range(N)]
+    jobs = {}
+    helper = {}
     for s in range(N):
-        ring = [(s + k) % N for k in range(1, N)]
-        if mate[s] is None:
-            direct[s] = [[d for d in ring if not same[s][d]], [d for d in ring if same[s][d] and d not in nxt[s]]]
-            continue
-        direct[s] = [[mate[s]] + [d for d in ring if same[s][d] and mate[d] is None and d not in nxt[s]]]
-        for d in ring:
-            if mate[d] is not None and same[s][d]:
-                first[s].append(chip_of(topo, cores[d]))
-                relays[first[s][-1]].append((s, [mate[d]] + ([d] if d not in nxt[s] else [])))
-            elif mate[d] is None and not same[s][d]:
-                first[s].append(mchip[d])
-                relays[mchip[d]].append((s, [d]))
-    for ch, lst in relays.items():
-        lst.sort(key=lambda e: (serves[ch] - e[0]) % N)
-    alias = {}
-    for ch, r in home.items():
-        used = [s for s, _ in relays[ch]]
-        alias[ch] = idx([s for s in range(N) if s != r and s not in used][0], r)
+        over = [d for d in ring[s] if d not in plane[s]][0]
+        gates = [[], []]
+        for c in chips[chip_of(topo, cores[s])]:
+            if c != cores[s] and topo.may_write(c, cores[over]):
+                gates[topo.die(c) != topo.die(cores[s])].append(c)
+        for kind, u in PARTS:
+            c = gates[(s + u) % 2][0] if kind == "q" else gates[1][1]
+            helper[(s, kind, u)] = c
+            jobs.setdefault(c, []).append((kind, u, far[s]))
     order = []
     for d in range(N):
-        soon = [s for s in range(N) if s not in early[d] and any(d in l for l in direct[s])]
-        soon.sort(key=lambda s: (s != mate[d], (d - s) % N))
-        late = [s for s in range(N) if s != d and s not in early[d] and s not in soon]
-        late.sort(key=lambda s: (not same[s][d], (d - s) % N))
-        items = [(d, 0), (d, 1)] + [(s, w) for w in range(2) for s in early[d]]
-        for s in soon + late:
-            items += [(s, 0), (s, 1)]
-        order.append(items)
-    _memo["p"] = {"home": home, "mate": mate, "serves": serves, "gate": gate, "same": same, "direct": direct,
-                  "first": first, "relays": relays, "alias": alias, "order": order, "nxt": nxt, "early": early}
+        rest = [s for s in range(N) if s != d and s not in early[d]]
+        rest.sort(key=lambda s: (far[s].index(d), (d - s) % N))
+        items = [(s, w) for s in [d] + early[d] for w in range(2)] + [(rest[0], 0)]
+        for a, b in zip(rest, rest[1:]):
+            items += [(b, 0), (a, 1)]
+        order.append(items + [(rest[-1], 1)])
+    _memo["p"] = {"nxt": nxt, "early": early, "jobs": jobs, "helper": helper, "order": order}
     return _memo["p"]
-
-
-def side(s, w):
-    return (s + w) % 2
 
 
 def rank_program(g, core, T, topo):
     P = plan(topo, T.cores)
-    ch = chip_of(topo, core)
-    if ch not in P["serves"]:
-        return
-    if T.rank_of(core) is None:
-        helper_program(g, core, T, topo, P, ch)
-    else:
-        rank_core_program(g, core, T, topo, P, ch)
+    if T.rank_of(core) is not None:
+        rank_core_program(g, core, T, topo, P)
+    elif core in P["jobs"]:
+        helper_program(g, core, T, topo, P)
 
 
-def view(T, kind, i, u):
-    b = T["%s%d_%d" % (kind, i, u)]
-    return b[:].bitcast(dt.uint8) if kind == "q" else b[:]
+def cspan(T, c, n=1):
+    return T.cq[:, c * W:(c + n) * W]
 
 
-def transfer(core, T, topo, kind, s, u, src, dests, mask):
-    ids = []
-    for c, _ in dests:
-        rid, pid = topo.addr(c, core)
-        ids.append(DstId(rid=rid, pnc=pid))
-    return RemoteDMATransfer(dst_ids=ids, dma_engine_mask=mask, remote_sem=T.sem["a%s%d_%d" % (kind, s, u)],
-                             srcs=[src], dsts=[v for _, v in dests])
+def pspan(T, c, t=0, n=KT):
+    return T.cp[:, (KT * c + t) * W:(KT * c + t + n) * W]
 
 
-def off_chip(topo, cores):
-    return topo.mask(cores[0], [c for c in cores if topo.same_plane(cores[0], c)][0])
+def raw(v, kind):
+    return v.bitcast(dt.uint8) if kind == "q" else v
 
 
-def helper_jobs(P, ch):
-    jobs = {}
-    gate = P["gate"][ch]
-    me = P["home"].get(ch)
-
-    def add(c, *job):
-        jobs.setdefault(c, []).append(job)
-
-    if me is not None:
-        others = [(me + k) % N for k in range(1, N)]
-        same = [d for d in others if P["same"][me][d] and d not in P["nxt"][me]]
-        cross = [d for d in others if not P["same"][me][d]]
-        for w in range(2):
-            groups = [[("rank", d) for d in l] for l in P["direct"][me]] + [[("relay", c) for c in P["first"][me]]]
-            add(gate[side(me, w)][0], "send", "q", w, [grp for grp in groups if grp])
-        add(gate[side(me, 1)][1], "send", "p", 0, [[("rank", d) for d in cross]])
-        if same:
-            add(gate[side(me, 0)][1], "send", "p", 0, [[("rank", d) for d in same]])
-    for w in range(2):
-        for s, ranks in P["relays"][ch]:
-            add(gate[side(s, w)][1], "relay", "q", w, s, ranks)
-    return jobs
+def kept(T, kind, u, i=0):
+    return raw(T["%s%d_%d" % (kind, i, u)][:], kind)
 
 
-def handed(P, ch, kind, w):
-    return [c for c, js in sorted(helper_jobs(P, ch).items()) if any(j[:3] == ("send", kind, w) for j in js)]
+def landing(T, P, kind, s, u, d):
+    near = P["early"][d]
+    if s == near[0] and (kind, u) == ("q", 0):
+        return raw(cspan(T, KT, 2), "q")
+    if s in near and kind == "p":
+        return pspan(T, 1 + near.index(s))
+    return kept(T, kind, u, idx(s, d))
 
 
-def helper_program(g, core, T, topo, P, ch):
+def transfer(core, T, topo, kind, s, u, src, dest, view, mask):
+    rid, pid = topo.addr(dest, core)
+    return RemoteDMATransfer(dst_ids=[DstId(rid=rid, pnc=pid)], dma_engine_mask=mask,
+                             remote_sem=T.sem["a%s%d_%d" % (kind, s, u)], srcs=[src], dsts=[view])
+
+
+def off_chip(topo, core):
+    return topo.mask(core, [c for c in range(SIM) if topo.same_plane(core, c)][0])
+
+
+def on_chip(topo, core, helper):
+    return topo.mask(core, helper) & ~off_chip(topo, core)
+
+
+def helper_program(g, core, T, topo, P):
     cores = T.cores
-    me = P["serves"][ch]
-    off = off_chip(topo, cores)
-    sent = [0]
-
-    def call(trs):
-        g.remote_dma_fused(trs, local_sem=T.sem.sent)
-        sent[0] += ones(off) * len(trs)
-
-    for job in helper_jobs(P, ch).get(core, []):
-        if job[0] == "send":
-            _, kind, w, groups = job
-            src = view(T, kind, P["alias"][ch], w)
-            g.wait_ge(T.sem["a%s%d_%d" % (kind, me, w)], ones(off))
-            for grp in groups:
-                dests = []
-                for to, d in grp:
-                    if to == "rank":
-                        dests.append((cores[d], view(T, kind, idx(me, d), w)))
-                    else:
-                        dests.append((P["gate"][d][side(me, w)][1], view(T, kind, idx(me, P["serves"][d]), w)))
-                call([transfer(core, T, topo, kind, me, w, src, dests, topo.mask(core, dests[0][0]) & off)])
-        else:
-            _, kind, w, s, ranks = job
-            src = view(T, kind, idx(s, me), w)
-            g.wait_ge(T.sem["a%s%d_%d" % (kind, s, w)], ones(off))
-            trs = []
-            for d in ranks:
-                m = topo.mask(core, cores[d])
-                trs.append(transfer(core, T, topo, kind, s, w, src, [(cores[d], view(T, kind, idx(s, d), w))],
-                                    m if m == off else m & ~off))
-            call(trs)
-    if sent[0]:
-        g.wait_ge(T.sem.sent, sent[0])
+    me = [r for r in range(N) if chip_of(topo, cores[r]) == chip_of(topo, core)][0]
+    off = off_chip(topo, core)
+    sent = 0
+    for kind, u, ranks in P["jobs"][core]:
+        g.wait_ge(T.sem["a%s%d_%d" % (kind, me, u)], ones(on_chip(topo, cores[me], core)))
+        for d in ranks:
+            g.remote_dma_fused([transfer(core, T, topo, kind, me, u, kept(T, kind, u), cores[d], landing(T, P, kind, me, u, d), off)],
+                               local_sem=T.sem.sent)
+            sent += ones(off)
+    g.wait_ge(T.sem.sent, sent)
 
 
-def rank_core_program(g, core, T, topo, P, ch):
+def rank_core_program(g, core, T, topo, P):
     cores = T.cores
     me = T.rank_of(core)
-    al = P["alias"][ch]
-    off = off_chip(topo, cores)
+    off = off_chip(topo, core)
     full = ones(off)
     S = T.sem
     items = P["order"][me]
-    lead = P["early"][me][0]
-    nxt = P["nxt"][me]
-
-    def cspan(c, n=1):
-        return T.cq[:, c * W:(c + n) * W]
-
-    def pspan(c, n=1):
-        return T.cp[:, 2 * c * W:2 * (c + n) * W]
-
-    def ptile(c, h):
-        return T.cp[:, (2 * c + h) * W:(2 * c + h + 1) * W]
+    near = P["early"][me]
 
     def xcols(t):
         return T.xs[:, (t % 2) * 4 * W:(t % 2 + 1) * 4 * W]
@@ -238,51 +166,35 @@ def rank_core_program(g, core, T, topo, P, ch):
     g.scalar.dma_start(T.wp[:], T.ws[:]).then_inc(S.wld, 16)
     for t in range(KT):
         g.vector.wait_ge(S["x%d" % t], 16)
-        g.vector.quantize_mx(cspan(t), ptile(t // 2, t % 2), xcols(t)).then_inc(S.qz, 1)
-    g.sync.wait_ge(S.qz, 1)
-    xload(g.sync, 2)
-    g.scalar.wait_ge(S.qz, 2)
-    xload(g.scalar, 3)
+        g.vector.quantize_mx(cspan(T, t), pspan(T, 0, t, 1), xcols(t)).then_inc(S.qz, 1)
+    for t in (2, 3):
+        q = (g.sync, g.scalar)[t % 2]
+        q.wait_ge(S.qz, t - 1)
+        xload(q, t)
 
     fo = {}
-    for kind, w in (("q", 0), ("p", 0), ("q", 1)):
-        g.wait_ge(S.qz, 2 if (kind, w) == ("q", 0) else KT)
-        if kind == "q":
-            src, sem = cspan(2 * w, 2).bitcast(dt.uint8), "fo%d" % w
-        else:
-            src, sem = pspan(0, 2), "fp0"
-        hs = handed(P, ch, kind, w)
-        trs = [transfer(core, T, topo, kind, me, w, src, [(h, view(T, kind, al, w)) for h in hs], topo.mask(core, hs[0]) & ~off)]
-        dests = []
-        for d in nxt:
-            land = view(T, kind, idx(me, d), w)
-            if P["early"][d][0] == me and (kind, w) == ("q", 0):
-                land = cspan(KT, 2).bitcast(dt.uint8)
-            if P["early"][d][0] == me and kind == "p":
-                land = pspan(2, 2)
-            dests.append((cores[d], land))
-        trs.append(transfer(core, T, topo, kind, me, w, src, dests, off))
-        g.remote_dma_fused(trs, local_sem=S[sem])
-        fo[sem] = full * len(trs)
+    for kind, u, first in CALLS:
+        g.wait_ge(S.qz, 2 if (kind, u) == ("q", 0) else KT)
+        src = raw(cspan(T, 2 * u, 2), "q") if kind == "q" else pspan(T, 0)
+        d = P["nxt"][me][0 if first else 1]
+        trs = [transfer(core, T, topo, kind, me, u, src, cores[d], landing(T, P, kind, me, u, d), off)]
+        fo[(kind, u)] = fo.get((kind, u), 0) + full
+        if first:
+            h = P["helper"][(me, kind, u)]
+            m = on_chip(topo, core, h)
+            trs.append(transfer(core, T, topo, kind, me, u, src, h, kept(T, kind, u), m))
+            fo[(kind, u)] += ones(m)
+        g.remote_dma_fused(trs, local_sem=S["f%s%d" % (kind, u)])
 
     srcs = [s for s, w in items if w == 0]
     done = [s for s, w in items if w == 1]
+    pos = {x: i for i, x in enumerate(items)}
     bank = {s: k % NBANK for k, s in enumerate(srcs)}
-    last = {s: 2 * items.index((s, 1)) + 2 for s in srcs}
-    pl, before = {}, {}
-    for i, (s, w) in enumerate(items):
-        if s == me:
-            pl[i] = w
-        elif s == lead:
-            pl[i] = 2 + w
-    queue = [i for i in range(2)]
-    for i, (s, w) in enumerate(items):
-        if s == lead:
-            queue.append(i)
-        elif s != me:
-            before[i] = queue.pop(0)
-            pl[i] = pl[before[i]]
-            queue.append(i)
+    last = {s: 2 * pos[(s, 1)] + 2 for s in srcs}
+    before = {s: srcs[k - NPL] for k, s in enumerate(srcs) if k >= NPL}
+    pslot = {s: k % NPL for k, s in enumerate(srcs)}
+    prev = {x: items[i - NSLOT // 2] for i, x in enumerate(items) if i >= NSLOT // 2}
+    slot = {x: 2 * (i % (NSLOT // 2)) for i, x in enumerate(items)}
 
     uses, need, pneed = {}, {}, {}
 
@@ -291,52 +203,42 @@ def rank_core_program(g, core, T, topo, P, ch):
         uses[sem] = uses.get(sem, 0) + 16
         return (sem, uses[sem])
 
-    for i, (s, w) in enumerate(items):
+    for s, w in items:
         if s == me:
             continue
-        if s == lead:
-            pneed[i] = ("ap%d_0" % s, full)
-        else:
-            g.sync.wait_ge(S.mm, 2 * before[i] + 2)
-            if before[i] < 2:
-                g.sync.wait_ge(S.fp0, fo["fp0"])
+        if s in near:
+            pneed[s] = ("ap%d_0" % s, full)
+        elif w == 0:
+            g.sync.wait_ge(S.mm, last[before[s]])
+            if before[s] == me:
+                g.sync.wait_ge(S.fp0, fo[("p", 0)])
             g.sync.wait_ge(S["ap%d_0" % s], full)
-            pneed[i] = load("pl%d" % pl[i], pspan(pl[i]), T["p%d_0" % idx(s, me)][:, 2 * w * W:2 * (w + 1) * W])
-        n = 2 * i
-        if s == lead and w == 0:
-            need[n] = need[n + 1] = ("aq%d_%d" % (s, w), full)
+            pneed[s] = load("pl%d" % pslot[s], pspan(T, pslot[s]), kept(T, "p", 0, idx(s, me)))
+        if (s, w) not in prev:
+            need[(s, w)] = ("aq%d_%d" % (s, w), full)
             continue
-        src = T["q%d_%d" % (idx(s, me), w)]
-        pieces = [(0, 2)] if n % NSLOT + 1 < NSLOT else [(0, 1), (1, 1)]
         g.sync.wait_ge(S["aq%d_%d" % (s, w)], full)
-        for h, m in pieces:
-            lo, hi = n + h - NSLOT, n + h + m - NSLOT
-            if hi > 0:
-                g.sync.wait_ge(S.mm, hi)
-            for u in range(2):
-                if max(lo, 2 * u) < min(hi, 2 * u + 2):
-                    g.sync.wait_ge(S["fo%d" % u], fo["fo%d" % u])
-            c = (n + h) % NSLOT
-            nd = load("ls%d" % c, cspan(c, m).bitcast(dt.uint8), src[:, h * W:(h + m) * W].bitcast(dt.uint8))
-            for b in range(m):
-                need[n + h + b] = nd
+        r, v = prev[(s, w)]
+        g.sync.wait_ge(S.mm, 2 * pos[(r, v)] + 2)
+        if r == me:
+            g.sync.wait_ge(S["fq%d" % v], fo[("q", v)])
+        c = slot[(s, w)]
+        need[(s, w)] = load("ls%d" % c, raw(cspan(T, c, 2), "q"), kept(T, "q", w, idx(s, me)))
 
     g.tensor.wait_ge(S.wld, 32)
-    for i, (s, w) in enumerate(items):
+    for s, w in items:
         k = srcs.index(s)
         if s == me:
             g.tensor.wait_ge(S.qz, 2 * w + 2)
         else:
-            g.tensor.wait_ge(S[pneed[i][0]], pneed[i][1])
+            if w == 0:
+                g.tensor.wait_ge(S[pneed[s][0]], pneed[s][1])
+            g.tensor.wait_ge(S[need[(s, w)][0]], need[(s, w)][1])
         if w == 0 and k >= NBANK:
             g.tensor.wait_ge(S.ev, done.index(srcs[k - NBANK]) + 1)
-        for h in range(2):
-            t = 2 * w + h
-            n = 2 * i + h
-            if s != me and (h == 0 or need[n] != need[n - 1]):
-                g.tensor.wait_ge(S[need[n][0]], need[n][1])
+        for t in (2 * w, 2 * w + 1):
             g.tensor.matmul_mx(T.ps[:, 512 * bank[s]:512 * bank[s] + W], T.wq[:, t * W:(t + 1) * W], T.wp[:, t * W:(t + 1) * W],
-                               cspan(n % NSLOT), ptile(pl[i], h), t == 0, t == KT - 1).then_inc(S.mm, 1)
+                               cspan(T, slot[(s, w)] + t - 2 * w), pspan(T, pslot[s], t, 1), t == 0, t == KT - 1).then_inc(S.mm, 1)
 
     for k, j in enumerate(done):
         c = k % NY
@@ -349,5 +251,5 @@ def rank_core_program(g, core, T, topo, P, ch):
 
     for c in range(NY):
         g.scalar.wait_ge(S["ys%d" % c], 16 * len([k for k in range(N) if k % NY == c]))
-    for sem in fo:
-        g.wait_ge(S[sem], fo[sem])
+    for part in fo:
+        g.wait_ge(S["f%s%d" % part], fo[part])

from concourse.bass import DstId, RemoteDMATransfer
from concourse.mybir import dt

N = 10
KT = 4
W = 128
SIM = 256
NSLOT = 6
NPL = 3
NY = 2
NBANK = 8
NEAR = 2

PARTS = [("q", 0), ("p", 0), ("q", 1)]
CALLS = [("q", 0, True), ("p", 0, True), ("q", 1, True), ("p", 0, False), ("q", 0, False), ("q", 1, False)]

SCRATCH = {
    "xs": ("sbuf", [128, 2 * 4 * W], "bfloat16"),
    "wq": ("sbuf", [128, KT * W], "float8_e4m3fn_x4"),
    "wp": ("sbuf", [128, KT * W], "uint8"),
    "cq": ("sbuf", [128, NSLOT * W], "float8_e4m3fn_x4"),
    "cp": ("sbuf", [128, NPL * KT * W], "uint8"),
    "yb": ("sbuf", [128, NY * W], "float32"),
    "ps": ("psum", [128, 512 * NBANK], "float32"),
}
for _i in range(N - 1):
    for _w in range(2):
        SCRATCH["q%d_%d" % (_i, _w)] = ("dram", [128, 2 * W], "float8_e4m3fn_x4")
    SCRATCH["p%d_0" % _i] = ("dram", [128, KT * W], "uint8")

SEMAPHORES = (["x%d" % t for t in range(KT)] + ["wld", "qz", "mm", "ev", "sent"] + ["f%s%d" % p for p in PARTS]
              + ["ls%d" % c for c in range(NSLOT)] + ["pl%d" % c for c in range(NPL)] + ["ys%d" % c for c in range(NY)]
              + ["a%s%d_%d" % (k, s, u) for s in range(N) for k, u in PARTS])


def ones(mask):
    return bin(mask).count("1")


def chip_of(topo, c):
    return (topo.host(c), topo.chip(c))


def idx(s, d):
    return (s - d - 1) % N


_memo = {}


def plan(topo, cores):
    if "p" in _memo:
        return _memo["p"]
    chips = {}
    for c in range(SIM):
        chips.setdefault(chip_of(topo, c), []).append(c)
    ring = [[(s + k) % N for k in range(1, N)] for s in range(N)]
    plane = [[d for d in ring[s] if topo.same_plane(cores[s], cores[d])] for s in range(N)]
    nxt = [plane[s][:NEAR] for s in range(N)]
    early = [[[s for s in range(N) if nxt[s][k] == d][0] for k in range(NEAR)] for d in range(N)]
    third = [plane[s][NEAR:NEAR + 1] for s in range(N)]
    far = [third[s] + [d for d in ring[s] if d not in nxt[s] + third[s]] for s in range(N)]
    jobs = {}
    helper = {}
    for s in range(N):
        over = [d for d in ring[s] if d not in plane[s]][0]
        gates = [[], []]
        for c in chips[chip_of(topo, cores[s])]:
            if c != cores[s] and topo.may_write(c, cores[over]):
                gates[topo.die(c) != topo.die(cores[s])].append(c)
        for kind, u in PARTS:
            c = gates[(s + u) % 2][0] if kind == "q" else gates[1][1]
            helper[(s, kind, u)] = c
            jobs.setdefault(c, []).append((kind, u, far[s]))
    order = []
    for d in range(N):
        rest = [s for s in range(N) if s != d and s not in early[d]]
        rest.sort(key=lambda s: (far[s].index(d), (d - s) % N))
        items = [(s, w) for s in [d] + early[d] for w in range(2)] + [(rest[0], 0)]
        for a, b in zip(rest, rest[1:]):
            items += [(b, 0), (a, 1)]
        order.append(items + [(rest[-1], 1)])
    _memo["p"] = {"nxt": nxt, "early": early, "jobs": jobs, "helper": helper, "order": order}
    return _memo["p"]


def rank_program(g, core, T, topo):
    P = plan(topo, T.cores)
    if T.rank_of(core) is not None:
        rank_core_program(g, core, T, topo, P)
    elif core in P["jobs"]:
        helper_program(g, core, T, topo, P)


def cspan(T, c, n=1):
    return T.cq[:, c * W:(c + n) * W]


def pspan(T, c, t=0, n=KT):
    return T.cp[:, (KT * c + t) * W:(KT * c + t + n) * W]


def raw(v, kind):
    return v.bitcast(dt.uint8) if kind == "q" else v


def kept(T, kind, u, i=0):
    return raw(T["%s%d_%d" % (kind, i, u)][:], kind)


def landing(T, P, kind, s, u, d):
    near = P["early"][d]
    if s == near[0] and (kind, u) == ("q", 0):
        return raw(cspan(T, KT, 2), "q")
    if s in near and kind == "p":
        return pspan(T, 1 + near.index(s))
    return kept(T, kind, u, idx(s, d))


def transfer(core, T, topo, kind, s, u, src, dest, view, mask):
    rid, pid = topo.addr(dest, core)
    return RemoteDMATransfer(dst_ids=[DstId(rid=rid, pnc=pid)], dma_engine_mask=mask,
                             remote_sem=T.sem["a%s%d_%d" % (kind, s, u)], srcs=[src], dsts=[view])


def off_chip(topo, core):
    return topo.mask(core, [c for c in range(SIM) if topo.same_plane(core, c)][0])


def on_chip(topo, core, helper):
    return topo.mask(core, helper) & ~off_chip(topo, core)


def helper_program(g, core, T, topo, P):
    cores = T.cores
    me = [r for r in range(N) if chip_of(topo, cores[r]) == chip_of(topo, core)][0]
    off = off_chip(topo, core)
    sent = 0
    for kind, u, ranks in P["jobs"][core]:
        g.wait_ge(T.sem["a%s%d_%d" % (kind, me, u)], ones(on_chip(topo, cores[me], core)))
        for d in ranks:
            g.remote_dma_fused([transfer(core, T, topo, kind, me, u, kept(T, kind, u), cores[d], landing(T, P, kind, me, u, d), off)],
                               local_sem=T.sem.sent)
            sent += ones(off)
    g.wait_ge(T.sem.sent, sent)


def rank_core_program(g, core, T, topo, P):
    cores = T.cores
    me = T.rank_of(core)
    off = off_chip(topo, core)
    full = ones(off)
    S = T.sem
    items = P["order"][me]
    near = P["early"][me]

    def xcols(t):
        return T.xs[:, (t % 2) * 4 * W:(t % 2 + 1) * 4 * W]

    def xload(q, t):
        q.dma_start(xcols(t), T.x[:, t * 4 * W:(t + 1) * 4 * W]).then_inc(S["x%d" % t], 16)

    xload(g.sync, 0)
    xload(g.scalar, 1)
    g.sync.dma_start(T.wq[:].bitcast(dt.uint8), T.wc[:]).then_inc(S.wld, 16)
    g.scalar.dma_start(T.wp[:], T.ws[:]).then_inc(S.wld, 16)
    for t in range(KT):
        g.vector.wait_ge(S["x%d" % t], 16)
        g.vector.quantize_mx(cspan(T, t), pspan(T, 0, t, 1), xcols(t)).then_inc(S.qz, 1)
    for t in (2, 3):
        q = (g.sync, g.scalar)[t % 2]
        q.wait_ge(S.qz, t - 1)
        xload(q, t)

    fo = {}
    for kind, u, first in CALLS:
        g.wait_ge(S.qz, 2 if (kind, u) == ("q", 0) else KT)
        src = raw(cspan(T, 2 * u, 2), "q") if kind == "q" else pspan(T, 0)
        d = P["nxt"][me][0 if first else 1]
        trs = [transfer(core, T, topo, kind, me, u, src, cores[d], landing(T, P, kind, me, u, d), off)]
        fo[(kind, u)] = fo.get((kind, u), 0) + full
        if first:
            h = P["helper"][(me, kind, u)]
            m = on_chip(topo, core, h)
            trs.append(transfer(core, T, topo, kind, me, u, src, h, kept(T, kind, u), m))
            fo[(kind, u)] += ones(m)
        g.remote_dma_fused(trs, local_sem=S["f%s%d" % (kind, u)])

    srcs = [s for s, w in items if w == 0]
    done = [s for s, w in items if w == 1]
    pos = {x: i for i, x in enumerate(items)}
    bank = {s: k % NBANK for k, s in enumerate(srcs)}
    last = {s: 2 * pos[(s, 1)] + 2 for s in srcs}
    before = {s: srcs[k - NPL] for k, s in enumerate(srcs) if k >= NPL}
    pslot = {s: k % NPL for k, s in enumerate(srcs)}
    prev = {x: items[i - NSLOT // 2] for i, x in enumerate(items) if i >= NSLOT // 2}
    slot = {x: 2 * (i % (NSLOT // 2)) for i, x in enumerate(items)}

    uses, need, pneed = {}, {}, {}

    def load(sem, out, in_):
        g.sync.dma_start(out, in_).then_inc(S[sem], 16)
        uses[sem] = uses.get(sem, 0) + 16
        return (sem, uses[sem])

    for s, w in items:
        if s == me:
            continue
        if s in near:
            pneed[s] = ("ap%d_0" % s, full)
        elif w == 0:
            g.sync.wait_ge(S.mm, last[before[s]])
            if before[s] == me:
                g.sync.wait_ge(S.fp0, fo[("p", 0)])
            g.sync.wait_ge(S["ap%d_0" % s], full)
            pneed[s] = load("pl%d" % pslot[s], pspan(T, pslot[s]), kept(T, "p", 0, idx(s, me)))
        if (s, w) not in prev:
            need[(s, w)] = ("aq%d_%d" % (s, w), full)
            continue
        g.sync.wait_ge(S["aq%d_%d" % (s, w)], full)
        r, v = prev[(s, w)]
        g.sync.wait_ge(S.mm, 2 * pos[(r, v)] + 2)
        if r == me:
            g.sync.wait_ge(S["fq%d" % v], fo[("q", v)])
        c = slot[(s, w)]
        need[(s, w)] = load("ls%d" % c, raw(cspan(T, c, 2), "q"), kept(T, "q", w, idx(s, me)))

    g.tensor.wait_ge(S.wld, 32)
    for s, w in items:
        k = srcs.index(s)
        if s == me:
            g.tensor.wait_ge(S.qz, 2 * w + 2)
        else:
            if w == 0:
                g.tensor.wait_ge(S[pneed[s][0]], pneed[s][1])
            g.tensor.wait_ge(S[need[(s, w)][0]], need[(s, w)][1])
        if w == 0 and k >= NBANK:
            g.tensor.wait_ge(S.ev, done.index(srcs[k - NBANK]) + 1)
        for t in (2 * w, 2 * w + 1):
            g.tensor.matmul_mx(T.ps[:, 512 * bank[s]:512 * bank[s] + W], T.wq[:, t * W:(t + 1) * W], T.wp[:, t * W:(t + 1) * W],
                               cspan(T, slot[(s, w)] + t - 2 * w), pspan(T, pslot[s], t, 1), t == 0, t == KT - 1).then_inc(S.mm, 1)

    for k, j in enumerate(done):
        c = k % NY
        g.vector.wait_ge(S.mm, last[j])
        if k >= NY:
            g.vector.wait_ge(S["ys%d" % c], 16 * (k // NY))
        g.vector.tensor_copy(T.yb[:, c * W:(c + 1) * W], T.ps[:, 512 * bank[j]:512 * bank[j] + W]).then_inc(S.ev, 1)
        g.scalar.wait_ge(S.ev, k + 1)
        g.scalar.dma_start(T.y[:, j * W:(j + 1) * W], T.yb[:, c * W:(c + 1) * W]).then_inc(S["ys%d" % c], 16)

    for c in range(NY):
        g.scalar.wait_ge(S["ys%d" % c], 16 * len([k for k in range(N) if k % NY == c]))
    for part in fo:
        g.wait_ge(S["f%s%d" % part], fo[part])
